import numpy as np
import ml_dtypes


def mxq(x, axis, fmt="e4m3"):
    dtype, down = {"e4m3": (ml_dtypes.float8_e4m3fn, 7), "e5m2": (ml_dtypes.float8_e5m2, 14)}[fmt]
    v = np.moveaxis(np.asarray(x, np.float32).astype(ml_dtypes.bfloat16).astype(np.float64), axis, -1)
    blocks = v.reshape(v.shape[:-1] + (-1, 32))
    amax = np.abs(blocks).max(-1, keepdims=True)
    byte = np.maximum(np.where(amax > 0, np.frexp(amax)[1] - 1 + 127, 0) - down, 1)
    scale = np.exp2(byte - 127.0)
    codes = (blocks / scale).astype(np.float32).astype(dtype).astype(np.float64)
    return np.moveaxis((codes * scale).reshape(v.shape), -1, axis)


WIDE = False


def mx_kscale(k):
    if not WIDE:
        return np.ones(k)
    levels = np.array([30, -30])
    if k % 512:
        return np.exp2(np.random.permutation(np.resize(levels, k // 32))).repeat(32)
    a = np.empty((k // 512, 16))
    for p in range(k // 512):
        a[p, :8] = np.random.permutation(np.resize(levels, 8))
        for g in range(8):
            far = levels[np.abs(levels - a[p, g]) >= 10]
            a[p, g + 8] = far[np.random.randint(len(far))]
    return np.exp2(a.ravel()).repeat(32)


def f64(x):
    return np.asarray(x).astype(np.float64)


def striped(idx):
    return np.tile(np.asarray(idx).reshape(-1, 16).T, (8, 1)).astype(np.uint16)


def unstriped(offs):
    return offs[:16].T.reshape(-1).astype(np.int64)


E2M1 = np.array([0.0, 0.5, 1.0, 1.5, 2.0, 3.0, 4.0, 6.0, -0.0, -0.5, -1.0, -1.5, -2.0, -3.0, -4.0, -6.0])


def pack_weight(w, fmt):
    k, n = w.shape
    w = f64(np.asarray(w, np.float32).astype(ml_dtypes.bfloat16)).reshape(k // 32, 32, n)
    amax = np.abs(w).max(1)
    if fmt in ("e4m3", "e5m2"):
        byte = np.frexp(amax)[1] - 1 + 127 - (7 if fmt == "e4m3" else 14)
    else:
        mant, ex = np.frexp(amax / 6.0)
        byte = np.where(mant > 0.5, ex, ex - 1) + 127
    byte = np.clip(np.where(amax > 0, byte, 1), 1, 254)
    scaled = (w * np.exp2(127.0 - byte)[:, None, :]).reshape(k, n).astype(np.float32)
    by_word = np.ascontiguousarray(scaled.reshape(k // 512, 128, 4, n).transpose(0, 1, 3, 2))
    if fmt in ("e4m3", "e5m2"):
        words = by_word.astype(ml_dtypes.float8_e4m3fn if fmt == "e4m3" else ml_dtypes.float8_e5m2).view(np.uint8)
    else:
        c = by_word.astype(ml_dtypes.float4_e2m1fn).view(np.uint8) & 0xF
        words = (c[..., 0::2] | (c[..., 1::2] << 4)).reshape(k // 512, 128, 2 * n)
    return np.ascontiguousarray(words), np.ascontiguousarray(byte.astype(np.uint8).reshape(k // 512, 16, n))


def unpack_weight(words, scales, fmt):
    g, _, n = scales.shape
    words = np.ascontiguousarray(words).reshape(g, 128, n, -1)
    if fmt in ("e4m3", "e5m2"):
        vals = words.view(ml_dtypes.float8_e4m3fn if fmt == "e4m3" else ml_dtypes.float8_e5m2).astype(np.float64)
    else:
        nib = np.empty((g, 128, n, 4), np.uint8)
        nib[..., 0::2] = words & 0xF
        nib[..., 1::2] = words >> 4
        vals = E2M1[nib]
    vals = vals * np.repeat(np.exp2(scales.astype(np.float64) - 127.0), 8, axis=1)[..., None]
    return vals.transpose(0, 1, 3, 2).reshape(g * 512, n)


K, T, J, I, R, Q = 512, 512, 256, 256, 512, 1024


def setup_inputs():
    n = np.random.standard_normal
    idx = np.random.permutation(T)[:J]
    idx2 = np.random.permutation(T)[:I]
    idx3 = np.random.permutation(Q)[:I]
    fk = mx_kscale(K)
    fr = mx_kscale(R)
    xtp = pack_weight(n((K, T)) / fk[:, None], "e4m3")
    wap = pack_weight(n((K, R)) * 0.5 / np.sqrt(K) * fk[:, None] * fr, "e2m1")
    wbp = pack_weight(n((K, R)) * 1 / np.sqrt(K) * fk[:, None] / fr, "e5m2")
    return {
        "xt_words": xtp[0],
        "xt_scales": xtp[1],
        "wa_words": wap[0],
        "wa_scales": wap[1],
        "wb_words": wbp[0],
        "wb_scales": wbp[1],
        "old": (10.0 * n((J, Q))).astype(np.float32),
        "offs": striped(idx),
        "offs2": striped(idx2),
        "offs3": striped(idx3),
    }


def reference(xt_words, xt_scales, wa_words, wa_scales, wb_words, wb_scales, old, offs, offs2, offs3):
    idx = unstriped(offs)
    idx2 = unstriped(offs2)
    idx3 = unstriped(offs3)
    xtu = unpack_weight(xt_words, xt_scales, "e4m3")
    wau = unpack_weight(wa_words, wa_scales, "e2m1")
    wbu = unpack_weight(wb_words, wb_scales, "e5m2")
    xtidxg = xtu[:, idx]
    za = wau.T @ xtidxg
    ya1 = np.pad(za, ((0, 0), (1, 0)))[:, :J]
    ha = za - 0.6 * ya1
    xtidx2g = xtu[:, idx2]
    zb = wbu.T @ xtidx2g
    kb1 = np.max(zb, axis=1, keepdims=True)
    hb = np.maximum(zb - 0.4 * kb1, 0.0)
    haq = mxq(ha, 0, "e4m3")
    hbq = mxq(hb, 0, "e5m2")
    a0 = haq.T @ hbq
    pp = np.zeros((J, Q))
    pp[:, idx3] = a0
    y = 0.04 * (pp - f64(old))
    return y

@@ -1,0 +1,209 @@
+from contextlib import ExitStack
+
+import concourse.mybir as mybir
+
+K, T, J, I, R, Q = 512, 512, 256, 256, 512, 1024
+FLOPS = 2 * K * R * J + 2 * K * R * I + 2 * R * J * I
+
+F32 = mybir.dt.float32
+BF16 = mybir.dt.bfloat16
+I32 = mybir.dt.int32
+U32 = mybir.dt.uint32
+U16 = mybir.dt.uint16
+U8 = mybir.dt.uint8
+E4M3 = mybir.dt.float8_e4m3fn_x4
+E5M2 = mybir.dt.float8_e5m2_x4
+E2M1 = mybir.dt.float4_e2m1fn_x4
+ALU = mybir.AluOpType
+ACT = mybir.ActivationFunctionType
+
+P = 128
+PACK = 4
+RUN = 8
+HALF = 128
+PIECES = (((0, 512), (512, 1024)), ((0, 512), (512, 768), (768, 1024)))
+
+
+def load_scale_rows(queues, plane, scales):
+    rows = scales[0].bitcast(I32)
+    for quad in range(4):
+        four = rows[4 * quad : 4 * quad + 4, :].unsqueeze(0).to_broadcast([8, 4, rows.shape[1]])
+        queues[quad].dma_start(out=plane[32 * quad : 32 * (quad + 1), :], in_=four)
+
+
+def deal(nc, dst, src, run):
+    nc.scalar.copy(
+        out=dst.rearrange("p (t b u) -> p t b u", t=PACK, u=run),
+        in_=src.rearrange("p (b t u) -> p t b u", t=PACK, u=run),
+    )
+
+
+def tile_list_meet_lagged_peakgated_placed_kernel(
+    tc, xt_words, xt_scales, wa_words, wa_scales, wb_words, wb_scales, old, offs, offs2, offs3, out
+):
+    nc = tc.nc
+    with ExitStack() as ctx:
+        lists = ctx.enter_context(tc.tile_pool(name="lists", bufs=1))
+        keep = ctx.enter_context(tc.tile_pool(name="keep", bufs=1))
+        psum = ctx.enter_context(tc.psum_pool(name="psum", bufs=1))
+
+        list_a = lists.tile([P, J // 16], U16, name="list_a")
+        list_b = lists.tile([P, I // 16], U16, name="list_b")
+        list_q = lists.tile([P, I // 16], U16, name="list_q")
+
+        xt_w = keep.tile([P, T], I32, name="xt_w", align_bytes=64)
+        xt_s = keep.tile([P, T // 4], I32, name="xt_s", align_bytes=64)
+        wb_raw = keep.tile([P, R], I32, name="wb_raw", tag="stage0", align_bytes=64)
+        wa_raw = keep.tile([P, R // 2], I32, name="wa_raw", tag="stage1", align_bytes=64)
+        wb_sraw = keep.tile([P, R // 4], I32, name="wb_sraw", align_bytes=64)
+        wa_sraw = keep.tile([P, R // 4], I32, name="wa_sraw", align_bytes=64)
+
+        nc.sync.dma_start(list_b[:], offs2)
+        load_scale_rows([nc.scalar, nc.sync, nc.scalar, nc.sync], xt_s, xt_scales)
+        nc.scalar.dma_start(out=xt_w[:], in_=xt_words[0].rearrange("p c t -> p (c t)").bitcast(I32))
+        nc.sync.dma_start(list_a[:], offs)
+        nc.scalar.dma_start(out=wb_raw[:], in_=wb_words[0].rearrange("p c t -> p (c t)").bitcast(I32))
+        load_scale_rows([nc.sync] * 4, wb_sraw, wb_scales)
+        nc.gpsimd.dma_start(out=wa_raw[:], in_=wa_words[0].bitcast(I32))
+        load_scale_rows([nc.sync] * 4, wa_sraw, wa_scales)
+        nc.sync.dma_start(list_q[:], offs3)
+
+        lagged = keep.tile([P, PACK + J * PACK], F32, name="lagged", align_bytes=64)
+        nc.vector.memset(lagged[:, 0:PACK], 0.0)
+        boards = [keep.tile([P, Q], F32, name="board%d" % h) for h in range(2)]
+        for board in boards:
+            nc.vector.memset(board[:], 0.0)
+
+        xb_w = keep.tile([P, I], U32, name="xb_w", align_bytes=64)
+        xb_s = keep.tile([P, I], U8, name="xb_s", align_bytes=64)
+        xa_w = keep.tile([P, J], U32, name="xa_w", align_bytes=64)
+        xa_s = keep.tile([P, J], U8, name="xa_s", align_bytes=64)
+        nc.vector.tensor_copy(xb_s[:], xt_s[:].bitcast(U8).indirect(list_b[:]))
+        nc.vector.tensor_copy(xa_s[:], xt_s[:].bitcast(U8).indirect(list_a[:]))
+        nc.vector.tensor_copy(xb_w[:], xt_w[:].bitcast(U32).indirect(list_b[:]))
+        nc.vector.tensor_copy(xa_w[:], xt_w[:].bitcast(U32).indirect(list_a[:]))
+
+        wb_w = keep.tile([P, R], U32, name="wb_w", align_bytes=64)
+        wb_s = keep.tile([P, R], U8, name="wb_s", align_bytes=64)
+        wa_w = keep.tile([P, 2 * R], U8, name="wa_w", align_bytes=64)
+        wa_s = keep.tile([P, R], U8, name="wa_s", align_bytes=64)
+        deal(nc, wb_w[:], wb_raw[:].bitcast(U32), RUN)
+        deal(nc, wa_w[:].bitcast(U16), wa_raw[:].bitcast(U16), RUN)
+        deal(nc, wb_s[:].bitcast(U32), wb_sraw[:].bitcast(U32), RUN // 4)
+        deal(nc, wa_s[:].bitcast(U32), wa_sraw[:].bitcast(U32), RUN // 4)
+
+        olds = []
+        for h in range(2):
+            prev = keep.tile([P, Q], F32, name="old%d" % h, tag="stage%d" % h, align_bytes=64)
+            nc.sync.dma_start(out=prev[:], in_=old[h * P : (h + 1) * P, :])
+            olds.append(prev)
+
+        floor_b = keep.tile([P, PACK], F32, name="floor_b")
+        scaled = keep.tile([P, PACK, I], BF16, name="scaled")
+        hb_rows = keep.tile([P, PACK, I], BF16, name="hb_rows", align_bytes=64)
+        for t in range(PACK):
+            zb = psum.tile([P, I], F32, name="zb%d" % t)
+            cols = slice(t * P, (t + 1) * P)
+            nc.tensor.matmul_mx(
+                out=zb[:],
+                lhsT=wb_w[:, cols].bitcast(E5M2),
+                lhsT_scale=wb_s[:, cols],
+                rhs=xb_w[:].bitcast(E4M3),
+                rhs_scale=xb_s[:],
+                start=True,
+                stop=True,
+            )
+            nc.vector.tensor_scalar(scaled[:, t, :], zb[:], -0.4, None, ALU.mult, ALU.min, accum_out=floor_b[:, t : t + 1])
+            nc.scalar.activation(hb_rows[:, t, :], zb[:], ACT.Relu, bias=floor_b[:, t : t + 1])
+
+        for h in range(2):
+            za = psum.tile([P, PACK, HALF], F32, name="za%d" % h)
+            cols = slice(h * HALF, (h + 1) * HALF)
+            for t in range(PACK):
+                nc.tensor.matmul_mx(
+                    out=za[:, t, :],
+                    lhsT=wa_w[:, 2 * t * P : 2 * (t + 1) * P].bitcast(E2M1),
+                    lhsT_scale=wa_s[:, t * P : (t + 1) * P],
+                    rhs=xa_w[:, cols].bitcast(E4M3),
+                    rhs_scale=xa_s[:, cols],
+                    start=True,
+                    stop=True,
+                )
+            lo = PACK + h * HALF * PACK
+            nc.scalar.copy(
+                out=lagged[:, lo : lo + HALF * PACK].rearrange("p (j t) -> p j t", t=PACK),
+                in_=za[:].rearrange("p t j -> p j t"),
+            )
+
+        hb_in = keep.tile([P, I * PACK], BF16, name="hb_in", tag="hb_in", align_bytes=64)
+        hb_w = keep.tile([P, I], U32, name="hb_w", align_bytes=64)
+        hb_s = keep.tile([P, I], U8, name="hb_s", align_bytes=64)
+        ha_w = keep.tile([P, J], U32, name="ha_w", align_bytes=64)
+        ha_s = keep.tile([P, J], U8, name="ha_s", align_bytes=64)
+
+        def lag(h, tag):
+            lo = h * HALF * PACK
+            ha_in = keep.tile([P, HALF * PACK], BF16, name="ha_in%d" % h, tag=tag, align_bytes=64)
+            nc.vector.scalar_tensor_tensor(
+                out=ha_in[:],
+                in0=lagged[:, lo : lo + HALF * PACK],
+                scalar=-0.6,
+                in1=lagged[:, PACK + lo : PACK + lo + HALF * PACK],
+                op0=ALU.mult,
+                op1=ALU.add,
+            )
+            return ha_in
+
+        def quantise_a(h, ha_in):
+            cols = slice(h * HALF, (h + 1) * HALF)
+            nc.vector.quantize_mx(
+                out=ha_w[:, cols].bitcast(E4M3),
+                scales=ha_s[:, cols],
+                in_=ha_in[:],
+            )
+
+        def meet(h):
+            cols = slice(h * HALF, (h + 1) * HALF)
+            a0 = psum.tile([P, I], F32, name="a0_%d" % h)
+            nc.tensor.matmul_mx(
+                out=a0[:],
+                lhsT=ha_w[:, cols].bitcast(E4M3),
+                lhsT_scale=ha_s[:, cols],
+                rhs=hb_w[:].bitcast(E5M2),
+                rhs_scale=hb_s[:],
+                start=True,
+                stop=True,
+            )
+            return a0
+
+        nc.vector.tensor_copy(
+            out=hb_in[:].rearrange("p (c i t) -> p c t i", i=4, t=PACK),
+            in_=hb_rows[:].rearrange("p t (c i) -> p c t i", i=4),
+        )
+        ha_in = lag(0, "ha_in")
+        nc.vector.quantize_mx(out=hb_w[:].bitcast(E5M2), scales=hb_s[:], in_=hb_in[:])
+        quantise_a(0, ha_in)
+        scores0 = keep.tile([P, I], F32, name="scores0")
+        a0 = meet(0)
+        nc.scalar.activation(scores0[:], a0[:], ACT.Copy, scale=0.04)
+        nc.scalar.activation(boards[0][:].indirect(list_q[:]), scores0[:], ACT.Copy)
+        quantise_a(1, lag(1, "hb_in"))
+        a0 = meet(1)
+        res = keep.tile([P, 2, Q], F32, name="res")
+        seam = slice((Q - HALF) // 2, (Q + HALF) // 2)
+        nc.vector.tensor_scalar(res[:, :, seam], a0[:].rearrange("p (e i) -> p e i", e=2), 0.04, None, ALU.mult)
+        nc.vector.tensor_copy(boards[1][:].indirect(list_q[:, 0:8]), res[:, 0, seam])
+        nc.scalar.activation(boards[1][:].indirect(list_q[:, 8:16]), res[:, 1, seam], ACT.Copy)
+
+        for h in range(2):
+            for lo, hi in PIECES[h]:
+                cols = slice(lo, hi)
+                nc.vector.scalar_tensor_tensor(
+                    out=res[:, h, cols],
+                    in0=olds[h][:, cols],
+                    scalar=-0.04,
+                    in1=boards[h][:, cols],
+                    op0=ALU.mult,
+                    op1=ALU.add,
+                )
+                nc.sync.dma_start(out=out[h * P : (h + 1) * P, cols], in_=res[:, h, cols])

@@ -56,7 +56,7 @@ def tile_list_meet_lagged_peakgated_placed_kernel(
         wb_raw = keep.tile([P, R], I32, name="wb_raw", tag="stage0", align_bytes=64)
         wa_raw = keep.tile([P, R // 2], I32, name="wa_raw", tag="stage1", align_bytes=64)
         wb_sraw = keep.tile([P, R // 4], I32, name="wb_sraw", align_bytes=64)
-        wa_sraw = keep.tile([P, R // 4], I32, name="wa_sraw", align_bytes=64)
+        wa_sraw = keep.tile([P, R // 4], I32, name="wa_sraw", tag="stage2", align_bytes=64)
 
         nc.sync.dma_start(list_b[:], offs2)
         load_scale_rows([nc.scalar, nc.sync, nc.scalar, nc.sync], xt_s, xt_scales)
@@ -64,8 +64,8 @@ def tile_list_meet_lagged_peakgated_placed_kernel(
         nc.sync.dma_start(list_a[:], offs)
         nc.scalar.dma_start(out=wb_raw[:], in_=wb_words[0].rearrange("p c t -> p (c t)").bitcast(I32))
         load_scale_rows([nc.sync] * 4, wb_sraw, wb_scales)
-        nc.gpsimd.dma_start(out=wa_raw[:], in_=wa_words[0].bitcast(I32))
-        load_scale_rows([nc.sync] * 4, wa_sraw, wa_scales)
+        nc.sync.dma_start(out=wa_raw[:], in_=wa_words[0].bitcast(I32))
+        load_scale_rows([nc.sync, nc.sync, nc.sync, nc.gpsimd], wa_sraw, wa_scales)
         nc.sync.dma_start(list_q[:], offs3)
 
         lagged = keep.tile([P, PACK + J * PACK], F32, name="lagged", align_bytes=64)
@@ -79,8 +79,8 @@ def tile_list_meet_lagged_peakgated_placed_kernel(
         xa_w = keep.tile([P, J], U32, name="xa_w", align_bytes=64)
         xa_s = keep.tile([P, J], U8, name="xa_s", align_bytes=64)
         nc.vector.tensor_copy(xb_s[:], xt_s[:].bitcast(U8).indirect(list_b[:]))
-        nc.vector.tensor_copy(xa_s[:], xt_s[:].bitcast(U8).indirect(list_a[:]))
         nc.vector.tensor_copy(xb_w[:], xt_w[:].bitcast(U32).indirect(list_b[:]))
+        nc.vector.tensor_copy(xa_s[:], xt_s[:].bitcast(U8).indirect(list_a[:]))
         nc.vector.tensor_copy(xa_w[:], xt_w[:].bitcast(U32).indirect(list_a[:]))
 
         wb_w = keep.tile([P, R], U32, name="wb_w", align_bytes=64)
@@ -88,8 +88,8 @@ def tile_list_meet_lagged_peakgated_placed_kernel(
         wa_w = keep.tile([P, 2 * R], U8, name="wa_w", align_bytes=64)
         wa_s = keep.tile([P, R], U8, name="wa_s", align_bytes=64)
         deal(nc, wb_w[:], wb_raw[:].bitcast(U32), RUN)
-        deal(nc, wa_w[:].bitcast(U16), wa_raw[:].bitcast(U16), RUN)
         deal(nc, wb_s[:].bitcast(U32), wb_sraw[:].bitcast(U32), RUN // 4)
+        deal(nc, wa_w[:].bitcast(U16), wa_raw[:].bitcast(U16), RUN)
         deal(nc, wa_s[:].bitcast(U32), wa_sraw[:].bitcast(U32), RUN // 4)
 
         olds = []
@@ -100,7 +100,7 @@ def tile_list_meet_lagged_peakgated_placed_kernel(
 
         floor_b = keep.tile([P, PACK], F32, name="floor_b")
         scaled = keep.tile([P, PACK, I], BF16, name="scaled")
-        hb_rows = keep.tile([P, PACK, I], BF16, name="hb_rows", align_bytes=64)
+        hb_rows = keep.tile([P, PACK, I], BF16, name="hb_rows", tag="stage2", align_bytes=64)
         for t in range(PACK):
             zb = psum.tile([P, I], F32, name="zb%d" % t)
             cols = slice(t * P, (t + 1) * P)

@@ -21,7 +21,7 @@ P = 128
 PACK = 4
 RUN = 8
 HALF = 128
-PIECES = (((0, 512), (512, 1024)), ((0, 512), (512, 768), (768, 1024)))
+PIECES = (((0, 512), (512, 1024)), ((0, 384), (384, 704), (704, 1024)))
 
 
 def load_scale_rows(queues, plane, scales):
@@ -102,7 +102,7 @@ def tile_list_meet_lagged_peakgated_placed_kernel(
         scaled = keep.tile([P, PACK, I], BF16, name="scaled")
         hb_rows = keep.tile([P, PACK, I], BF16, name="hb_rows", tag="stage2", align_bytes=64)
         for t in range(PACK):
-            zb = psum.tile([P, I], F32, name="zb%d" % t)
+            zb = psum.tile([P, I], F32, name="zb%d" % t, tag="zb%d" % t)
             cols = slice(t * P, (t + 1) * P)
             nc.tensor.matmul_mx(
                 out=zb[:],
@@ -141,36 +141,34 @@ def tile_list_meet_lagged_peakgated_placed_kernel(
         ha_w = keep.tile([P, J], U32, name="ha_w", align_bytes=64)
         ha_s = keep.tile([P, J], U8, name="ha_s", align_bytes=64)
 
-        def lag(h, tag):
-            lo = h * HALF * PACK
-            ha_in = keep.tile([P, HALF * PACK], BF16, name="ha_in%d" % h, tag=tag, align_bytes=64)
+        def lag(ha_in, h, lo, hi):
+            first = h * HALF * PACK
             nc.vector.scalar_tensor_tensor(
-                out=ha_in[:],
-                in0=lagged[:, lo : lo + HALF * PACK],
+                out=ha_in[:, lo * PACK : hi * PACK],
+                in0=lagged[:, first + lo * PACK : first + hi * PACK],
                 scalar=-0.6,
-                in1=lagged[:, PACK + lo : PACK + lo + HALF * PACK],
+                in1=lagged[:, first + (lo + 1) * PACK : first + (hi + 1) * PACK],
                 op0=ALU.mult,
                 op1=ALU.add,
             )
-            return ha_in
 
-        def quantise_a(h, ha_in):
-            cols = slice(h * HALF, (h + 1) * HALF)
+        def quantise_a(ha_in, h, lo, hi):
+            cols = slice(h * HALF + lo, h * HALF + hi)
             nc.vector.quantize_mx(
                 out=ha_w[:, cols].bitcast(E4M3),
                 scales=ha_s[:, cols],
-                in_=ha_in[:],
+                in_=ha_in[:, lo * PACK : hi * PACK],
             )
 
-        def meet(h):
-            cols = slice(h * HALF, (h + 1) * HALF)
-            a0 = psum.tile([P, I], F32, name="a0_%d" % h)
+        def meet(h, lo, hi, bank):
+            rows = slice(h * HALF, (h + 1) * HALF)
+            a0 = psum.tile([P, hi - lo], F32, name="a0", tag=bank)
             nc.tensor.matmul_mx(
                 out=a0[:],
-                lhsT=ha_w[:, cols].bitcast(E4M3),
-                lhsT_scale=ha_s[:, cols],
-                rhs=hb_w[:].bitcast(E5M2),
-                rhs_scale=hb_s[:],
+                lhsT=ha_w[:, rows].bitcast(E4M3),
+                lhsT_scale=ha_s[:, rows],
+                rhs=hb_w[:, lo:hi].bitcast(E5M2),
+                rhs_scale=hb_s[:, lo:hi],
                 start=True,
                 stop=True,
             )
@@ -180,18 +178,24 @@ def tile_list_meet_lagged_peakgated_placed_kernel(
             out=hb_in[:].rearrange("p (c i t) -> p c t i", i=4, t=PACK),
             in_=hb_rows[:].rearrange("p t (c i) -> p c t i", i=4),
         )
-        ha_in = lag(0, "ha_in")
+        ha_in = keep.tile([P, HALF * PACK], BF16, name="ha_in0", align_bytes=64)
+        lag(ha_in, 0, 0, HALF)
         nc.vector.quantize_mx(out=hb_w[:].bitcast(E5M2), scales=hb_s[:], in_=hb_in[:])
-        quantise_a(0, ha_in)
+        quantise_a(ha_in, 0, 0, HALF)
         scores0 = keep.tile([P, I], F32, name="scores0")
-        a0 = meet(0)
+        a0 = meet(0, 0, I, "a0_0")
         nc.scalar.activation(scores0[:], a0[:], ACT.Copy, scale=0.04)
         nc.scalar.activation(boards[0][:].indirect(list_q[:]), scores0[:], ACT.Copy)
-        quantise_a(1, lag(1, "hb_in"))
-        a0 = meet(1)
+
+        ha_in = keep.tile([P, HALF * PACK], BF16, name="ha_in1", tag="hb_in", align_bytes=64)
+        for step in (lag, quantise_a):
+            for lo in (0, HALF // 2):
+                step(ha_in, 1, lo, lo + HALF // 2)
         res = keep.tile([P, 2, Q], F32, name="res")
-        seam = slice((Q - HALF) // 2, (Q + HALF) // 2)
-        nc.vector.tensor_scalar(res[:, :, seam], a0[:].rearrange("p (e i) -> p e i", e=2), 0.04, None, ALU.mult)
+        seam = slice(PIECES[0][0][1] - HALF // 2, PIECES[0][0][1] + HALF // 2)
+        for e, bank in enumerate(("a0_1", "zb0")):
+            a0 = meet(1, e * HALF, (e + 1) * HALF, bank)
+            nc.vector.tensor_scalar(res[:, e, seam], a0[:], 0.04, None, ALU.mult)
         nc.vector.tensor_copy(boards[1][:].indirect(list_q[:, 0:8]), res[:, 0, seam])
         nc.scalar.activation(boards[1][:].indirect(list_q[:, 8:16]), res[:, 1, seam], ACT.Copy)
 

from contextlib import ExitStack

import concourse.mybir as mybir

K, T, J, I, R, Q = 512, 512, 256, 256, 512, 1024
FLOPS = 2 * K * R * J + 2 * K * R * I + 2 * R * J * I

F32 = mybir.dt.float32
BF16 = mybir.dt.bfloat16
I32 = mybir.dt.int32
U32 = mybir.dt.uint32
U16 = mybir.dt.uint16
U8 = mybir.dt.uint8
E4M3 = mybir.dt.float8_e4m3fn_x4
E5M2 = mybir.dt.float8_e5m2_x4
E2M1 = mybir.dt.float4_e2m1fn_x4
ALU = mybir.AluOpType
ACT = mybir.ActivationFunctionType

P = 128
PACK = 4
RUN = 8
HALF = 128
PIECES = (((0, 512), (512, 1024)), ((0, 384), (384, 704), (704, 1024)))


def load_scale_rows(queues, plane, scales):
    rows = scales[0].bitcast(I32)
    for quad in range(4):
        four = rows[4 * quad : 4 * quad + 4, :].unsqueeze(0).to_broadcast([8, 4, rows.shape[1]])
        queues[quad].dma_start(out=plane[32 * quad : 32 * (quad + 1), :], in_=four)


def deal(nc, dst, src, run):
    nc.scalar.copy(
        out=dst.rearrange("p (t b u) -> p t b u", t=PACK, u=run),
        in_=src.rearrange("p (b t u) -> p t b u", t=PACK, u=run),
    )


def tile_list_meet_lagged_peakgated_placed_kernel(
    tc, xt_words, xt_scales, wa_words, wa_scales, wb_words, wb_scales, old, offs, offs2, offs3, out
):
    nc = tc.nc
    with ExitStack() as ctx:
        lists = ctx.enter_context(tc.tile_pool(name="lists", bufs=1))
        keep = ctx.enter_context(tc.tile_pool(name="keep", bufs=1))
        psum = ctx.enter_context(tc.psum_pool(name="psum", bufs=1))

        list_a = lists.tile([P, J // 16], U16, name="list_a")
        list_b = lists.tile([P, I // 16], U16, name="list_b")
        list_q = lists.tile([P, I // 16], U16, name="list_q")

        xt_w = keep.tile([P, T], I32, name="xt_w", align_bytes=64)
        xt_s = keep.tile([P, T // 4], I32, name="xt_s", align_bytes=64)
        wb_raw = keep.tile([P, R], I32, name="wb_raw", tag="stage0", align_bytes=64)
        wa_raw = keep.tile([P, R // 2], I32, name="wa_raw", tag="stage1", align_bytes=64)
        wb_sraw = keep.tile([P, R // 4], I32, name="wb_sraw", align_bytes=64)
        wa_sraw = keep.tile([P, R // 4], I32, name="wa_sraw", tag="stage2", align_bytes=64)

        nc.sync.dma_start(list_b[:], offs2)
        load_scale_rows([nc.scalar, nc.sync, nc.scalar, nc.sync], xt_s, xt_scales)
        nc.scalar.dma_start(out=xt_w[:], in_=xt_words[0].rearrange("p c t -> p (c t)").bitcast(I32))
        nc.sync.dma_start(list_a[:], offs)
        nc.scalar.dma_start(out=wb_raw[:], in_=wb_words[0].rearrange("p c t -> p (c t)").bitcast(I32))
        load_scale_rows([nc.sync] * 4, wb_sraw, wb_scales)
        nc.sync.dma_start(out=wa_raw[:], in_=wa_words[0].bitcast(I32))
        load_scale_rows([nc.sync, nc.sync, nc.sync, nc.gpsimd], wa_sraw, wa_scales)
        nc.sync.dma_start(list_q[:], offs3)

        lagged = keep.tile([P, PACK + J * PACK], F32, name="lagged", align_bytes=64)
        nc.vector.memset(lagged[:, 0:PACK], 0.0)
        boards = [keep.tile([P, Q], F32, name="board%d" % h) for h in range(2)]
        for board in boards:
            nc.vector.memset(board[:], 0.0)

        xb_w = keep.tile([P, I], U32, name="xb_w", align_bytes=64)
        xb_s = keep.tile([P, I], U8, name="xb_s", align_bytes=64)
        xa_w = keep.tile([P, J], U32, name="xa_w", align_bytes=64)
        xa_s = keep.tile([P, J], U8, name="xa_s", align_bytes=64)
        nc.vector.tensor_copy(xb_s[:], xt_s[:].bitcast(U8).indirect(list_b[:]))
        nc.vector.tensor_copy(xb_w[:], xt_w[:].bitcast(U32).indirect(list_b[:]))
        nc.vector.tensor_copy(xa_s[:], xt_s[:].bitcast(U8).indirect(list_a[:]))
        nc.vector.tensor_copy(xa_w[:], xt_w[:].bitcast(U32).indirect(list_a[:]))

        wb_w = keep.tile([P, R], U32, name="wb_w", align_bytes=64)
        wb_s = keep.tile([P, R], U8, name="wb_s", align_bytes=64)
        wa_w = keep.tile([P, 2 * R], U8, name="wa_w", align_bytes=64)
        wa_s = keep.tile([P, R], U8, name="wa_s", align_bytes=64)
        deal(nc, wb_w[:], wb_raw[:].bitcast(U32), RUN)
        deal(nc, wb_s[:].bitcast(U32), wb_sraw[:].bitcast(U32), RUN // 4)
        deal(nc, wa_w[:].bitcast(U16), wa_raw[:].bitcast(U16), RUN)
        deal(nc, wa_s[:].bitcast(U32), wa_sraw[:].bitcast(U32), RUN // 4)

        olds = []
        for h in range(2):
            prev = keep.tile([P, Q], F32, name="old%d" % h, tag="stage%d" % h, align_bytes=64)
            nc.sync.dma_start(out=prev[:], in_=old[h * P : (h + 1) * P, :])
            olds.append(prev)

        floor_b = keep.tile([P, PACK], F32, name="floor_b")
        scaled = keep.tile([P, PACK, I], BF16, name="scaled")
        hb_rows = keep.tile([P, PACK, I], BF16, name="hb_rows", tag="stage2", align_bytes=64)
        for t in range(PACK):
            zb = psum.tile([P, I], F32, name="zb%d" % t, tag="zb%d" % t)
            cols = slice(t * P, (t + 1) * P)
            nc.tensor.matmul_mx(
                out=zb[:],
                lhsT=wb_w[:, cols].bitcast(E5M2),
                lhsT_scale=wb_s[:, cols],
                rhs=xb_w[:].bitcast(E4M3),
                rhs_scale=xb_s[:],
                start=True,
                stop=True,
            )
            nc.vector.tensor_scalar(scaled[:, t, :], zb[:], -0.4, None, ALU.mult, ALU.min, accum_out=floor_b[:, t : t + 1])
            nc.scalar.activation(hb_rows[:, t, :], zb[:], ACT.Relu, bias=floor_b[:, t : t + 1])

        for h in range(2):
            za = psum.tile([P, PACK, HALF], F32, name="za%d" % h)
            cols = slice(h * HALF, (h + 1) * HALF)
            for t in range(PACK):
                nc.tensor.matmul_mx(
                    out=za[:, t, :],
                    lhsT=wa_w[:, 2 * t * P : 2 * (t + 1) * P].bitcast(E2M1),
                    lhsT_scale=wa_s[:, t * P : (t + 1) * P],
                    rhs=xa_w[:, cols].bitcast(E4M3),
                    rhs_scale=xa_s[:, cols],
                    start=True,
                    stop=True,
                )
            lo = PACK + h * HALF * PACK
            nc.scalar.copy(
                out=lagged[:, lo : lo + HALF * PACK].rearrange("p (j t) -> p j t", t=PACK),
                in_=za[:].rearrange("p t j -> p j t"),
            )

        hb_in = keep.tile([P, I * PACK], BF16, name="hb_in", tag="hb_in", align_bytes=64)
        hb_w = keep.tile([P, I], U32, name="hb_w", align_bytes=64)
        hb_s = keep.tile([P, I], U8, name="hb_s", align_bytes=64)
        ha_w = keep.tile([P, J], U32, name="ha_w", align_bytes=64)
        ha_s = keep.tile([P, J], U8, name="ha_s", align_bytes=64)

        def lag(ha_in, h, lo, hi):
            first = h * HALF * PACK
            nc.vector.scalar_tensor_tensor(
                out=ha_in[:, lo * PACK : hi * PACK],
                in0=lagged[:, first + lo * PACK : first + hi * PACK],
                scalar=-0.6,
                in1=lagged[:, first + (lo + 1) * PACK : first + (hi + 1) * PACK],
                op0=ALU.mult,
                op1=ALU.add,
            )

        def quantise_a(ha_in, h, lo, hi):
            cols = slice(h * HALF + lo, h * HALF + hi)
            nc.vector.quantize_mx(
                out=ha_w[:, cols].bitcast(E4M3),
                scales=ha_s[:, cols],
                in_=ha_in[:, lo * PACK : hi * PACK],
            )

        def meet(h, lo, hi, bank):
            rows = slice(h * HALF, (h + 1) * HALF)
            a0 = psum.tile([P, hi - lo], F32, name="a0", tag=bank)
            nc.tensor.matmul_mx(
                out=a0[:],
                lhsT=ha_w[:, rows].bitcast(E4M3),
                lhsT_scale=ha_s[:, rows],
                rhs=hb_w[:, lo:hi].bitcast(E5M2),
                rhs_scale=hb_s[:, lo:hi],
                start=True,
                stop=True,
            )
            return a0

        nc.vector.tensor_copy(
            out=hb_in[:].rearrange("p (c i t) -> p c t i", i=4, t=PACK),
            in_=hb_rows[:].rearrange("p t (c i) -> p c t i", i=4),
        )
        ha_in = keep.tile([P, HALF * PACK], BF16, name="ha_in0", align_bytes=64)
        lag(ha_in, 0, 0, HALF)
        nc.vector.quantize_mx(out=hb_w[:].bitcast(E5M2), scales=hb_s[:], in_=hb_in[:])
        quantise_a(ha_in, 0, 0, HALF)
        scores0 = keep.tile([P, I], F32, name="scores0")
        a0 = meet(0, 0, I, "a0_0")
        nc.scalar.activation(scores0[:], a0[:], ACT.Copy, scale=0.04)
        nc.scalar.activation(boards[0][:].indirect(list_q[:]), scores0[:], ACT.Copy)

        ha_in = keep.tile([P, HALF * PACK], BF16, name="ha_in1", tag="hb_in", align_bytes=64)
        for step in (lag, quantise_a):
            for lo in (0, HALF // 2):
                step(ha_in, 1, lo, lo + HALF // 2)
        res = keep.tile([P, 2, Q], F32, name="res")
        seam = slice(PIECES[0][0][1] - HALF // 2, PIECES[0][0][1] + HALF // 2)
        for e, bank in enumerate(("a0_1", "zb0")):
            a0 = meet(1, e * HALF, (e + 1) * HALF, bank)
            nc.vector.tensor_scalar(res[:, e, seam], a0[:], 0.04, None, ALU.mult)
        nc.vector.tensor_copy(boards[1][:].indirect(list_q[:, 0:8]), res[:, 0, seam])
        nc.scalar.activation(boards[1][:].indirect(list_q[:, 8:16]), res[:, 1, seam], ACT.Copy)

        for h in range(2):
            for lo, hi in PIECES[h]:
                cols = slice(lo, hi)
                nc.vector.scalar_tensor_tensor(
                    out=res[:, h, cols],
                    in0=olds[h][:, cols],
                    scalar=-0.04,
                    in1=boards[h][:, cols],
                    op0=ALU.mult,
                    op1=ALU.add,
                )
                nc.sync.dma_start(out=out[h * P : (h + 1) * P, cols], in_=res[:, h, cols])
